import numpy as np
import ml_dtypes


def mxq(x, axis, fmt="e4m3"):
    dtype, down = {"e4m3": (ml_dtypes.float8_e4m3fn, 7), "e5m2": (ml_dtypes.float8_e5m2, 14)}[fmt]
    v = np.moveaxis(np.asarray(x, np.float32).astype(ml_dtypes.bfloat16).astype(np.float64), axis, -1)
    blocks = v.reshape(v.shape[:-1] + (-1, 32))
    amax = np.abs(blocks).max(-1, keepdims=True)
    byte = np.maximum(np.where(amax > 0, np.frexp(amax)[1] - 1 + 127, 0) - down, 1)
    scale = np.exp2(byte - 127.0)
    codes = (blocks / scale).astype(np.float32).astype(dtype).astype(np.float64)
    return np.moveaxis((codes * scale).reshape(v.shape), -1, axis)


WIDE = False


def mx_kscale(k):
    if not WIDE:
        return np.ones(k)
    levels = np.array([10, -10, 5, -5, 0])
    if k % 512:
        return np.exp2(np.random.permutation(np.resize(levels, k // 32))).repeat(32)
    a = np.empty((k // 512, 16))
    for p in range(k // 512):
        a[p, :8] = np.random.permutation(np.resize(levels, 8))
        for g in range(8):
            far = levels[np.abs(levels - a[p, g]) >= 10]
            a[p, g + 8] = far[np.random.randint(len(far))]
    return np.exp2(a.ravel()).repeat(32)


def f64(x):
    return np.asarray(x).astype(np.float64)


def striped(idx):
    return np.tile(idx.reshape(-1, 16).T, (8, 1)).astype(np.uint16)


def unstriped(offs):
    return offs[:16].T.reshape(-1).astype(np.int64)


def pack_weight(w):
    k, n = w.shape
    w = f64(np.asarray(w, np.float32).astype(ml_dtypes.bfloat16)).reshape(k // 32, 32, n)
    amax = np.abs(w).max(1)
    byte = np.clip(np.where(amax > 0, np.frexp(amax)[1] - 1 + 127 - 7, 1), 1, 254)
    scaled = (w * np.exp2(127.0 - byte)[:, None, :]).reshape(k, n).astype(np.float32)
    words = np.ascontiguousarray(scaled.reshape(k // 512, 128, 4, n).transpose(0, 1, 3, 2)).astype(ml_dtypes.float8_e4m3fn).view(np.uint8)
    return words, np.ascontiguousarray(byte.astype(np.uint8).reshape(k // 512, 16, n))


def unpack_weight(words, scales):
    g, p, n, _ = words.shape
    vals = np.ascontiguousarray(words).view(ml_dtypes.float8_e4m3fn).astype(np.float64) * np.repeat(np.exp2(scales.astype(np.float64) - 127.0), 8, axis=1)[..., None]
    return vals.transpose(0, 1, 3, 2).reshape(g * 512, n)


E2M1 = np.array([0.0, 0.5, 1.0, 1.5, 2.0, 3.0, 4.0, 6.0, -0.0, -0.5, -1.0, -1.5, -2.0, -3.0, -4.0, -6.0])


def pack_fp4(w):
    k, n = w.shape
    w = f64(np.asarray(w, np.float32).astype(ml_dtypes.bfloat16)).reshape(k // 32, 32, n)
    amax = np.abs(w).max(1)
    mant, ex = np.frexp(amax / 6.0)
    byte = np.clip(np.where(amax > 0, np.where(mant > 0.5, ex, ex - 1) + 127, 1), 1, 254)
    scaled = (w * np.exp2(127.0 - byte)[:, None, :]).reshape(k, n).astype(np.float32)
    c = np.ascontiguousarray(scaled.reshape(k // 512, 128, 4, n).transpose(0, 1, 3, 2)).astype(ml_dtypes.float4_e2m1fn).view(np.uint8) & 0xF
    words = (c[..., 0::2] | (c[..., 1::2] << 4)).reshape(k // 512, 128, 2 * n)
    return np.ascontiguousarray(words), np.ascontiguousarray(byte.astype(np.uint8).reshape(k // 512, 16, n))


def unpack_fp4(words, scales):
    g, _, n = scales.shape
    words = np.ascontiguousarray(words).reshape(g, 128, n, 2)
    nib = np.empty((g, 128, n, 4), np.uint8)
    nib[..., 0::2] = words & 0xF
    nib[..., 1::2] = words >> 4
    vals = E2M1[nib] * np.repeat(np.exp2(scales.astype(np.float64) - 127.0), 8, axis=1)[..., None]
    return vals.transpose(0, 1, 3, 2).reshape(g * 512, n)


K, T, S, N, H = 1024, 1024, 512, 128, 512


def setup_inputs():
    n = np.random.standard_normal
    s = mx_kscale(K)[:, None]
    u = mx_kscale(H)
    packed_xT = pack_weight(n((K, T)) * s)
    packed_w1 = pack_fp4(n((K, H)) / np.sqrt(K) / s)
    packed_w2 = pack_fp4(n((K, H)) / np.sqrt(K) / s)
    packed_w3 = pack_fp4(n((H, N)) / np.sqrt(H) / u[:, None])
    return {
        "x_words": packed_xT[0],
        "x_scales": packed_xT[1],
        "w1_words": packed_w1[0],
        "w1_scales": packed_w1[1],
        "w2_words": packed_w2[0],
        "w2_scales": packed_w2[1],
        "owat": (np.random.uniform(0.0, 1.0, (H, S))).astype(np.float32),
        "unit": (np.random.uniform(0.6, 1.4, (H, 1)) * u[:, None]).astype(np.float32),
        "w3_words": packed_w3[0],
        "w3_scales": packed_w3[1],
        "offs": striped(np.random.permutation(T)[:S]),
        "est": striped(np.random.permutation(S)),
        "nor": striped(np.random.permutation(S)),
    }


def reference(x_words, x_scales, w1_words, w1_scales, w2_words, w2_scales, owat, unit, w3_words, w3_scales, offs, est, nor):
    xq = unpack_weight(x_words, x_scales)[:, unstriped(offs)]
    hi = unpack_fp4(w1_words, w1_scales).T @ xq
    thk = np.log(np.exp(hi) + 1.0)
    pres = thk * (np.exp(-1.0 * f64(owat)))
    ui = unpack_fp4(w2_words, w2_scales).T @ xq
    uu = np.tanh(ui)
    ue = uu[:, unstriped(est)]
    epa = ue - uu
    un = uu[:, unstriped(nor)]
    epb = un - uu
    delta = np.sqrt((epa) ** 2 + 0.25 * ((epb) ** 2) + 0.05)
    zeta = pres / delta
    sig1 = zeta * epa - (0.5 * pres)
    se = sig1[:, unstriped(est)]
    sig2 = 0.25 * (zeta * epb)
    sn2 = sig2[:, unstriped(nor)]
    hid = f64(unit) * (se - sig1 + sn2 - sig2)
    return unpack_fp4(w3_words, w3_scales).T @ mxq(hid, 0, "e4m3")

@@ -1,0 +1,276 @@
+import math
+from contextlib import ExitStack
+
+import concourse.mybir as mybir
+from concourse.masks import make_identity
+
+K, T, S, H, N = 1024, 1024, 512, 512, 128
+FLOPS = 2 * (2 * K * H * S + H * N * S)
+
+F32 = mybir.dt.float32
+BF16 = mybir.dt.bfloat16
+I32 = mybir.dt.int32
+U32 = mybir.dt.uint32
+U16 = mybir.dt.uint16
+U8 = mybir.dt.uint8
+FP8X4 = mybir.dt.float8_e4m3fn_x4
+FP4X4 = mybir.dt.float4_e2m1fn_x4
+ALU = mybir.AluOpType
+ACT = mybir.ActivationFunctionType
+
+P = 128
+PASSES = K // 512
+TILES = H // P
+BLOCKS = S // P
+HALVES = 2
+HALF = S // HALVES
+LN_FLOOR = 2.0**-60
+SQ_SLOTS = {1: (1, 2), 2: (3, 0), 3: (2, 1)}
+INV_SLOT = (0, 1, 3, 0)
+
+
+def tile_picked_yseaic_div_p_kernel(
+    tc, x_words, x_scales, w1_words, w1_scales, w2_words, w2_scales, owat, unit, w3_words, w3_scales, offs, est, nor, out
+):
+    nc = tc.nc
+    with ExitStack() as ctx:
+        lists = ctx.enter_context(tc.tile_pool(name="lists", bufs=1))
+        keep = ctx.enter_context(tc.tile_pool(name="keep", bufs=1))
+        psum = ctx.enter_context(tc.psum_pool(name="psum", bufs=1))
+
+        def sbuf(name, shape, dtype=F32, tag=None):
+            return keep.tile(shape, dtype, name=name, tag=tag or name, align_bytes=64)
+
+        def bank(tag, name, shape):
+            return psum.tile(shape, F32, name=name, tag=tag)
+
+        def load_scale_rows(queue, plane, scales):
+            passes = scales.shape[0]
+            for q in range(4):
+                queue.dma_start(
+                    out=plane[32 * q : 32 * q + 4, :].bitcast(I32).rearrange("r (o c) -> r o c", o=passes),
+                    in_=scales.bitcast(I32)[:, 4 * q : 4 * q + 4, :].rearrange("o r c -> r o c"),
+                )
+
+        def load_fp4_words(queue, name, words):
+            passes, width = words.shape[0], words.shape[2]
+            tile = sbuf(name, [P, passes, width], U8)
+            queue.dma_start(out=tile[:].bitcast(I32), in_=words.bitcast(I32).rearrange("o p c -> p o c"))
+            return tile
+
+        offs_sb = lists.tile([P, S // 16], U16, name="offs_sb")
+        est_sb = lists.tile([P, S // 16], U16, name="est_sb")
+        nor_sb = lists.tile([P, S // 16], U16, name="nor_sb")
+
+        x_plane = sbuf("x_plane", [P, PASSES * T], U8)
+        w1_plane = sbuf("w1_plane", [P, PASSES * H], U8)
+        w2_plane = sbuf("w2_plane", [P, PASSES * H], U8)
+        w3_plane = sbuf("w3_plane", [P, N], U8)
+        for plane in (x_plane, w2_plane, w1_plane, w3_plane):
+            nc.vector.memset(plane[:].bitcast(I32), 0)
+
+        x_table = [sbuf(f"x_table{o}", [P, T], I32) for o in range(PASSES)]
+        water = [sbuf(f"water{g}", [P, 2, S]) for g in range(2)]
+
+        def load_x(o):
+            nc.sync.dma_start(out=x_table[o][:], in_=x_words[o].rearrange("p c r -> p (c r)").bitcast(I32))
+
+        load_x(0)
+        nc.sync.dma_start(offs_sb[:], offs)
+        load_scale_rows(nc.sync, x_plane, x_scales)
+        for g in range(2):
+            nc.sync.dma_start(out=water[g][:], in_=owat[256 * g : 256 * (g + 1), :].rearrange("(t p) s -> p t s", p=P))
+        load_x(1)
+        w2_sb = load_fp4_words(nc.sync, "w2_sb", w2_words)
+        load_scale_rows(nc.sync, w2_plane, w2_scales)
+        nc.sync.dma_start(est_sb[:], est)
+        nc.sync.dma_start(nor_sb[:], nor)
+        w1_sb = load_fp4_words(nc.sync, "w1_sb", w1_words)
+        load_scale_rows(nc.sync, w1_plane, w1_scales)
+        unit_sb = sbuf("unit_sb", [P, TILES])
+        with nc.allow_non_contiguous_dma(reason="one value a partition and feature tile"):
+            nc.sync.dma_start(out=unit_sb[:], in_=unit.rearrange("(t p) o -> p (t o)", p=P))
+        w3_sb = load_fp4_words(nc.sync, "w3_sb", w3_words)
+        load_scale_rows(nc.sync, w3_plane, w3_scales)
+
+        ident = sbuf("ident", [P, P])
+        make_identity(nc, ident[:])
+        minus_one = sbuf("minus_one", [P, HALF])
+        nc.gpsimd.memset(minus_one[:], -1.0)
+
+        x_codes = [sbuf(f"x_codes{o}", [P, S], U32) for o in range(PASSES)]
+        x_bytes = [sbuf(f"x_bytes{o}", [P, S], U8) for o in range(PASSES)]
+        nc.vector.tensor_copy(x_codes[0][:], x_table[0][:].bitcast(U32).indirect(offs_sb[:]))
+        for o in range(PASSES):
+            nc.vector.tensor_copy(x_bytes[o][:], x_plane[:, o * T : (o + 1) * T].indirect(offs_sb[:]))
+        nc.vector.tensor_copy(x_codes[1][:], x_table[1][:].bitcast(U32).indirect(offs_sb[:]))
+
+        vel = [sbuf(f"vel{t}", [P, 2 * S]) for t in range(TILES)]
+        for t in range(TILES):
+            nc.scalar.activation(vel[t][:, S:], water[t // 2][:, t % 2, :], ACT.Exp, bias=math.log(2.0), scale=-1.0)
+
+        ui = [bank(f"a{t}", f"ui{t}", [P, S]) for t in range(TILES)]
+        hi = [bank(f"b{t}", f"hi{t}", [P, S]) for t in range(TILES)]
+        for sums, words, plane in ((ui, w2_sb, w2_plane), (hi, w1_sb, w1_plane)):
+            for t in range(TILES):
+                for o in range(PASSES):
+                    nc.tensor.matmul_mx(
+                        out=sums[t][:],
+                        lhsT=words[:, o, 2 * P * t : 2 * P * (t + 1)].bitcast(FP4X4),
+                        lhsT_scale=plane[:, o * H + P * t : o * H + P * (t + 1)],
+                        rhs=x_codes[o][:].bitcast(FP8X4),
+                        rhs_scale=x_bytes[o][:],
+                        start=(o == 0),
+                        stop=(o == PASSES - 1),
+                    )
+
+        vel_plain = [sbuf(f"vel_plain{t}", [P, S]) for t in range(TILES)]
+        for t in range(TILES):
+            nc.scalar.activation(vel[t][:, :S], ui[t][:], ACT.Sigmoid, scale=2.0)
+            if t == 0:
+                nc.vector.tensor_copy(vel_plain[t][:], vel[t][:, :S])
+            else:
+                nc.sync.dma_start(out=vel_plain[t][:], in_=vel[t][:, :S])
+        shared = sbuf("shared", [P, TILES, S])
+        for t in range(TILES):
+            nc.scalar.activation(shared[:, t, :], hi[t][:], ACT.Sigmoid, scale=-1.0)
+
+        rate_e = [sbuf(f"rate_e{t}", [P, S]) for t in range(TILES)]
+        rate_n = [sbuf(f"rate_n{t}", [P, S]) for t in range(TILES)]
+        for t in range(TILES):
+            nc.vector.tensor_tensor(rate_e[t][:], vel[t][:].indirect(est_sb[:]), vel_plain[t][:], ALU.subtract)
+            nc.vector.tensor_tensor(rate_n[t][:], vel[t][:].indirect(nor_sb[:]), vel_plain[t][:], ALU.subtract)
+
+        def turn(dst, src, first, last):
+            nc.tensor.matmul(dst, lhsT=src, rhs=ident[:], start=first, stop=last, is_transpose=True)
+
+        strain = {}
+        inv_delta = {}
+        strength = {}
+        log_sig = sbuf("log_sig", [P, TILES, S])
+        hid_t = [sbuf(f"hid_t{g}", [P, 2, 2, P, 2], BF16) for g in range(HALVES)]
+
+        def strain_squared(t):
+            if t == 0:
+                sq_e, sq_n = sbuf("sq_e0", [P, S])[:], sbuf("sq_n0", [P, S])[:]
+            else:
+                sq_e, sq_n = (shared[:, slot, :] for slot in SQ_SLOTS[t])
+            nc.scalar.activation(sq_e, rate_e[t][:], ACT.Square, scale=2.0)
+            nc.scalar.activation(sq_n, rate_n[t][:], ACT.Square)
+            strain[t] = bank(f"a{t}", f"strain{t}", [P, BLOCKS, P])
+            for i, square in enumerate((sq_e, sq_n)):
+                for c in range(BLOCKS):
+                    turn(strain[t][:, c, :], square[:, P * c : P * (c + 1)], i == 0 and c == 0, i == 1 and c == BLOCKS - 1)
+
+        def ice_strength(t):
+            neg_thk = sbuf(f"neg_thk{t}", [P, S], tag="neg_thk")
+            strength[t] = sbuf(f"strength{t}", [P, S], tag=f"strength{t % 2}")
+            nc.vector.scalar_tensor_tensor(neg_thk[:], hi[t][:], -1.0, log_sig[:, t, :], ALU.mult, ALU.min)
+            nc.vector.scalar_tensor_tensor(strength[t][:], neg_thk[:], unit_sb[:, t : t + 1], vel[t][:, S:], ALU.mult, ALU.mult)
+
+        def inverse_delta(t):
+            slot = INV_SLOT[t]
+            nc.scalar.activation(shared[:, slot, :], strain[t][:].rearrange("p c f -> p (c f)"), ACT.Abs_reciprocal_sqrt, bias=0.05)
+            inv_delta[t] = bank(f"b{t}", f"inv_delta{t}", [P, S])
+            for c in range(BLOCKS):
+                turn(inv_delta[t][:, P * c : P * (c + 1)], shared[:, slot, P * c : P * (c + 1)], True, True)
+
+        stress = {}
+
+        def stresses(t):
+            sig1 = sbuf(f"sig1_{t}", [P, 2 * S])
+            sig2 = sbuf(f"sig2_{t}", [P, 2 * S])
+            nc.vector.tensor_tensor(sig1[:, S:], inv_delta[t][:], rate_e[t][:], ALU.mult)
+            nc.vector.tensor_tensor(sig2[:, S:], inv_delta[t][:], rate_n[t][:], ALU.mult)
+            nc.vector.scalar_tensor_tensor(sig1[:, :S], sig1[:, S:], -0.25, strength[t][:], ALU.add, ALU.mult)
+            nc.vector.scalar_tensor_tensor(sig2[:, :S], sig2[:, S:], 0.25, strength[t][:], ALU.mult, ALU.mult)
+            stress[t] = (sig1, sig2)
+
+        def divergence(t):
+            sig1, sig2 = stress[t]
+            last_tile = t == TILES - 1
+            pieces = HALVES if last_tile else 1
+            width = S // pieces
+            for g in range(pieces):
+                east = sbuf(f"east{t}_{g}", [P, width])
+                north = sbuf(f"north{t}_{g}", [P, width])
+                cols = slice(g * width // 16, (g + 1) * width // 16)
+                nc.scalar.activation(east[:], sig1[:].indirect(est_sb[:, cols]), ACT.Copy, scale=-1.0)
+                if last_tile:
+                    nc.vector.tensor_tensor(north[:], sig2[:].indirect(nor_sb[:, cols]), minus_one[:], ALU.mult)
+                else:
+                    nc.scalar.activation(north[:], sig2[:].indirect(nor_sb[:, cols]), ACT.Copy, scale=-1.0)
+                blocks = width // P
+                total = bank(f"a{t if g == 0 else 0}", f"hid{t}_{g}", [P, blocks, P])
+                terms = [(sig1, g * width), (sig2, g * width), (east, 0), (north, 0)]
+                for i, (term, base) in enumerate(terms):
+                    for c in range(blocks):
+                        turn(
+                            total[:, c, :],
+                            term[:, base + P * c : base + P * (c + 1)],
+                            i == 0 and c == 0,
+                            i == len(terms) - 1 and c == blocks - 1,
+                        )
+                for hh in range(HALVES // pieces):
+                    half = g + hh
+                    src = total[:, 2 * hh : 2 * hh + 2, :].rearrange("p c (m u e) -> p c u m e", u=2, e=2)
+                    dst = hid_t[half][:, :, :, 32 * t : 32 * (t + 1), :]
+                    if last_tile and half == 1:
+                        nc.vector.tensor_copy(dst, src)
+                    else:
+                        nc.scalar.copy(dst, src)
+
+        strain_squared(0)
+        nc.scalar.activation(log_sig[:], shared[:], ACT.Ln, bias=LN_FLOOR)
+        ice_strength(0)
+        inverse_delta(0)
+        ice_strength(1)
+        strain_squared(1)
+        stresses(0)
+        strain_squared(2)
+        inverse_delta(1)
+        ice_strength(2)
+        strain_squared(3)
+        inverse_delta(2)
+        stresses(1)
+        ice_strength(3)
+        inverse_delta(3)
+        divergence(0)
+        stresses(2)
+        divergence(1)
+        stresses(3)
+        divergence(2)
+        divergence(3)
+
+        for g in range(HALVES):
+            words = hid_t[g][:].rearrange("p c u m e -> p (c u m e)").bitcast(F32)
+            pairs = bank(f"b{g}", f"pairs{g}", [P, 2, 2, P])
+            for c in range(2):
+                for u in range(2):
+                    nc.tensor.transpose(pairs[:, c, u, :], words[:, (2 * c + u) * P : (2 * c + u + 1) * P], ident[:])
+            hid = sbuf(f"hid{g}", [P, HALF * 4], BF16)
+            dst = hid[:].bitcast(F32).rearrange("p (c j u) -> p c j u", c=2, u=2)
+            src = pairs[:].rearrange("p c u j -> p c j u")
+            if g == 0:
+                nc.scalar.copy(dst, src)
+            else:
+                nc.vector.tensor_copy(dst, src)
+            hid_codes = sbuf(f"hid_codes{g}", [P, HALF], U32)
+            hid_plane = sbuf(f"hid_plane{g}", [P, HALF], U8)
+            nc.vector.quantize_mx(out=hid_codes[:].bitcast(FP8X4), scales=hid_plane[:], in_=hid[:])
+            modes = bank(f"b{2 + g}", f"modes{g}", [P, HALF])
+            nc.tensor.matmul_mx(
+                out=modes[:],
+                lhsT=w3_sb[:, 0, :].bitcast(FP4X4),
+                lhsT_scale=w3_plane[:],
+                rhs=hid_codes[:].bitcast(FP8X4),
+                rhs_scale=hid_plane[:],
+                start=True,
+                stop=True,
+            )
+            result = sbuf(f"result{g}", [P, HALF])
+            if g == 0:
+                nc.scalar.copy(result[:], modes[:])
+            else:
+                nc.vector.tensor_copy(result[:], modes[:])
+            nc.sync.dma_start(out=out[:, g * HALF : (g + 1) * HALF], in_=result[:])

@@ -25,8 +25,8 @@ BLOCKS = S // P
 HALVES = 2
 HALF = S // HALVES
 LN_FLOOR = 2.0**-60
-SQ_SLOTS = {1: (1, 2), 2: (3, 0), 3: (2, 1)}
-INV_SLOT = (0, 1, 3, 0)
+SQ_N_SLOT = {2: 3, 3: 0}
+INV_SLOT = (0, 1, 2, 3)
 
 
 def tile_picked_yseaic_div_p_kernel(
@@ -95,42 +95,49 @@ def tile_picked_yseaic_div_p_kernel(
 
         ident = sbuf("ident", [P, P])
         make_identity(nc, ident[:])
-        minus_one = sbuf("minus_one", [P, HALF])
-        nc.gpsimd.memset(minus_one[:], -1.0)
 
         x_codes = [sbuf(f"x_codes{o}", [P, S], U32) for o in range(PASSES)]
         x_bytes = [sbuf(f"x_bytes{o}", [P, S], U8) for o in range(PASSES)]
         nc.vector.tensor_copy(x_codes[0][:], x_table[0][:].bitcast(U32).indirect(offs_sb[:]))
         for o in range(PASSES):
             nc.vector.tensor_copy(x_bytes[o][:], x_plane[:, o * T : (o + 1) * T].indirect(offs_sb[:]))
-        nc.vector.tensor_copy(x_codes[1][:], x_table[1][:].bitcast(U32).indirect(offs_sb[:]))
+        for g in range(HALVES):
+            nc.vector.tensor_copy(
+                x_codes[1][:, g * HALF : (g + 1) * HALF],
+                x_table[1][:].bitcast(U32).indirect(offs_sb[:, g * HALF // 16 : (g + 1) * HALF // 16]),
+            )
 
         vel = [sbuf(f"vel{t}", [P, 2 * S]) for t in range(TILES)]
         for t in range(TILES):
             nc.scalar.activation(vel[t][:, S:], water[t // 2][:, t % 2, :], ACT.Exp, bias=math.log(2.0), scale=-1.0)
 
-        ui = [bank(f"a{t}", f"ui{t}", [P, S]) for t in range(TILES)]
-        hi = [bank(f"b{t}", f"hi{t}", [P, S]) for t in range(TILES)]
-        for sums, words, plane in ((ui, w2_sb, w2_plane), (hi, w1_sb, w1_plane)):
-            for t in range(TILES):
-                for o in range(PASSES):
-                    nc.tensor.matmul_mx(
-                        out=sums[t][:],
-                        lhsT=words[:, o, 2 * P * t : 2 * P * (t + 1)].bitcast(FP4X4),
-                        lhsT_scale=plane[:, o * H + P * t : o * H + P * (t + 1)],
-                        rhs=x_codes[o][:].bitcast(FP8X4),
-                        rhs_scale=x_bytes[o][:],
-                        start=(o == 0),
-                        stop=(o == PASSES - 1),
-                    )
+        def product(sums, words, plane, t, cols):
+            for o in range(PASSES):
+                nc.tensor.matmul_mx(
+                    out=sums,
+                    lhsT=words[:, o, 2 * P * t : 2 * P * (t + 1)].bitcast(FP4X4),
+                    lhsT_scale=plane[:, o * H + P * t : o * H + P * (t + 1)],
+                    rhs=x_codes[o][:, cols].bitcast(FP8X4),
+                    rhs_scale=x_bytes[o][:, cols],
+                    start=(o == 0),
+                    stop=(o == PASSES - 1),
+                )
 
         vel_plain = [sbuf(f"vel_plain{t}", [P, S]) for t in range(TILES)]
+        for g in range(HALVES):
+            cols = slice(g * HALF, (g + 1) * HALF)
+            ui = bank(("a0", "b3")[g], f"ui0_{g}", [P, HALF])
+            product(ui[:], w2_sb, w2_plane, 0, cols)
+            nc.scalar.activation(vel[0][:, cols], ui[:], ACT.Sigmoid, scale=2.0)
+            nc.vector.tensor_copy(vel_plain[0][:, cols], vel[0][:, cols])
+        for t in range(1, TILES):
+            ui = bank(f"a{t}", f"ui{t}", [P, S])
+            product(ui[:], w2_sb, w2_plane, t, slice(0, S))
+            nc.scalar.activation(vel[t][:, :S], ui[:], ACT.Sigmoid, scale=2.0)
+            nc.sync.dma_start(out=vel_plain[t][:], in_=vel[t][:, :S])
+        hi = [bank(f"b{t}", f"hi{t}", [P, S]) for t in range(TILES)]
         for t in range(TILES):
-            nc.scalar.activation(vel[t][:, :S], ui[t][:], ACT.Sigmoid, scale=2.0)
-            if t == 0:
-                nc.vector.tensor_copy(vel_plain[t][:], vel[t][:, :S])
-            else:
-                nc.sync.dma_start(out=vel_plain[t][:], in_=vel[t][:, :S])
+            product(hi[t][:], w1_sb, w1_plane, t, slice(0, S))
         shared = sbuf("shared", [P, TILES, S])
         for t in range(TILES):
             nc.scalar.activation(shared[:, t, :], hi[t][:], ACT.Sigmoid, scale=-1.0)
@@ -148,117 +155,104 @@ def tile_picked_yseaic_div_p_kernel(
         inv_delta = {}
         strength = {}
         log_sig = sbuf("log_sig", [P, TILES, S])
-        hid_t = [sbuf(f"hid_t{g}", [P, 2, 2, P, 2], BF16) for g in range(HALVES)]
+        hid_t = [sbuf(f"hid_t{c}", [P, 2, P, 2], BF16) for c in range(BLOCKS)]
+        thickness = {}
 
         def strain_squared(t):
             if t == 0:
                 sq_e, sq_n = sbuf("sq_e0", [P, S])[:], sbuf("sq_n0", [P, S])[:]
+            elif t == 1:
+                sq_e, sq_n = shared[:, 1, :], shared[:, 2, :]
             else:
-                sq_e, sq_n = (shared[:, slot, :] for slot in SQ_SLOTS[t])
-            nc.scalar.activation(sq_e, rate_e[t][:], ACT.Square, scale=2.0)
-            nc.scalar.activation(sq_n, rate_n[t][:], ACT.Square)
+                sq_e, sq_n = vel_plain[5 - t][:], shared[:, SQ_N_SLOT[t], :]
+            if t < 2:
+                nc.scalar.activation(sq_e, rate_e[t][:], ACT.Square)
+            else:
+                nc.gpsimd.tensor_tensor(sq_e, rate_e[t][:], rate_e[t][:], ALU.mult)
+            nc.scalar.activation(sq_n, rate_n[t][:], ACT.Square, scale=0.5)
             strain[t] = bank(f"a{t}", f"strain{t}", [P, BLOCKS, P])
             for i, square in enumerate((sq_e, sq_n)):
                 for c in range(BLOCKS):
                     turn(strain[t][:, c, :], square[:, P * c : P * (c + 1)], i == 0 and c == 0, i == 1 and c == BLOCKS - 1)
 
+        def ice_thickness(t):
+            thickness[t] = sbuf(f"thickness{t}", [P, S])
+            if t == TILES - 1:
+                nc.vector.scalar_tensor_tensor(thickness[t][:], log_sig[:, t, :], -1.0, hi[t][:], ALU.mult, ALU.max)
+            else:
+                nc.vector.scalar_tensor_tensor(thickness[t][:], hi[t][:], -1.0, log_sig[:, t, :], ALU.mult, ALU.min)
+
         def ice_strength(t):
-            neg_thk = sbuf(f"neg_thk{t}", [P, S], tag="neg_thk")
-            strength[t] = sbuf(f"strength{t}", [P, S], tag=f"strength{t % 2}")
-            nc.vector.scalar_tensor_tensor(neg_thk[:], hi[t][:], -1.0, log_sig[:, t, :], ALU.mult, ALU.min)
-            nc.vector.scalar_tensor_tensor(strength[t][:], neg_thk[:], unit_sb[:, t : t + 1], vel[t][:, S:], ALU.mult, ALU.mult)
+            strength[t] = sbuf(f"strength{t}", [P, S]) if t < 2 else (rate_n[2], rate_e[2])[t - 2]
+            nc.vector.scalar_tensor_tensor(strength[t][:], thickness[t][:], unit_sb[:, t : t + 1], vel[t][:, S:], ALU.mult, ALU.mult)
 
         def inverse_delta(t):
             slot = INV_SLOT[t]
-            nc.scalar.activation(shared[:, slot, :], strain[t][:].rearrange("p c f -> p (c f)"), ACT.Abs_reciprocal_sqrt, bias=0.05)
+            nc.scalar.activation(
+                shared[:, slot, :], strain[t][:].rearrange("p c f -> p (c f)"), ACT.Abs_reciprocal_sqrt, bias=0.05, scale=4.0
+            )
             inv_delta[t] = bank(f"b{t}", f"inv_delta{t}", [P, S])
             for c in range(BLOCKS):
                 turn(inv_delta[t][:, P * c : P * (c + 1)], shared[:, slot, P * c : P * (c + 1)], True, True)
 
         stress = {}
 
-        def stresses(t):
+        def scaled_rates(t):
             sig1 = sbuf(f"sig1_{t}", [P, 2 * S])
             sig2 = sbuf(f"sig2_{t}", [P, 2 * S])
             nc.vector.tensor_tensor(sig1[:, S:], inv_delta[t][:], rate_e[t][:], ALU.mult)
-            nc.vector.tensor_tensor(sig2[:, S:], inv_delta[t][:], rate_n[t][:], ALU.mult)
-            nc.vector.scalar_tensor_tensor(sig1[:, :S], sig1[:, S:], -0.25, strength[t][:], ALU.add, ALU.mult)
-            nc.vector.scalar_tensor_tensor(sig2[:, :S], sig2[:, S:], 0.25, strength[t][:], ALU.mult, ALU.mult)
+            nc.vector.scalar_tensor_tensor(sig2[:, S:], inv_delta[t][:], 0.25, rate_n[t][:], ALU.mult, ALU.mult)
             stress[t] = (sig1, sig2)
+
+        def stresses(t):
+            sig1, sig2 = stress[t]
+            nc.vector.scalar_tensor_tensor(sig1[:, :S], sig1[:, S:], -0.25, strength[t][:], ALU.add, ALU.mult)
+            engine = nc.vector if t == TILES - 1 else nc.gpsimd
+            engine.tensor_tensor(sig2[:, :S], sig2[:, S:], strength[t][:], ALU.mult)
+
+        def round_hidden(t, c, total):
+            src = total.rearrange("p (m u e) -> p u m e", u=2, e=2)
+            nc.scalar.copy(hid_t[c][:, :, 32 * t : 32 * (t + 1), :], src)
 
         def divergence(t):
             sig1, sig2 = stress[t]
-            last_tile = t == TILES - 1
-            pieces = HALVES if last_tile else 1
-            width = S // pieces
-            for g in range(pieces):
-                east = sbuf(f"east{t}_{g}", [P, width])
-                north = sbuf(f"north{t}_{g}", [P, width])
-                cols = slice(g * width // 16, (g + 1) * width // 16)
-                nc.scalar.activation(east[:], sig1[:].indirect(est_sb[:, cols]), ACT.Copy, scale=-1.0)
-                if last_tile:
-                    nc.vector.tensor_tensor(north[:], sig2[:].indirect(nor_sb[:, cols]), minus_one[:], ALU.mult)
-                else:
-                    nc.scalar.activation(north[:], sig2[:].indirect(nor_sb[:, cols]), ACT.Copy, scale=-1.0)
-                blocks = width // P
-                total = bank(f"a{t if g == 0 else 0}", f"hid{t}_{g}", [P, blocks, P])
-                terms = [(sig1, g * width), (sig2, g * width), (east, 0), (north, 0)]
-                for i, (term, base) in enumerate(terms):
-                    for c in range(blocks):
-                        turn(
-                            total[:, c, :],
-                            term[:, base + P * c : base + P * (c + 1)],
-                            i == 0 and c == 0,
-                            i == len(terms) - 1 and c == blocks - 1,
-                        )
-                for hh in range(HALVES // pieces):
-                    half = g + hh
-                    src = total[:, 2 * hh : 2 * hh + 2, :].rearrange("p c (m u e) -> p c u m e", u=2, e=2)
-                    dst = hid_t[half][:, :, :, 32 * t : 32 * (t + 1), :]
-                    if last_tile and half == 1:
-                        nc.vector.tensor_copy(dst, src)
-                    else:
-                        nc.scalar.copy(dst, src)
+            east = sbuf(f"east{t}", [P, S])
+            north = sbuf(f"north{t}", [P, S])
+            nc.scalar.activation(east[:], sig1[:].indirect(est_sb[:]), ACT.Copy, scale=-1.0)
+            nc.scalar.activation(north[:], sig2[:].indirect(nor_sb[:]), ACT.Copy, scale=-1.0)
+            total = bank(f"a{t}", f"hid{t}", [P, BLOCKS, P])
+            terms = (sig1, sig2, east, north)
+            for i, term in enumerate(terms):
+                for c in range(BLOCKS):
+                    turn(total[:, c, :], term[:, P * c : P * (c + 1)], i == 0 and c == 0, i == len(terms) - 1 and c == BLOCKS - 1)
+            for c in range(BLOCKS):
+                round_hidden(t, c, total[:, c, :])
 
-        strain_squared(0)
-        nc.scalar.activation(log_sig[:], shared[:], ACT.Ln, bias=LN_FLOOR)
-        ice_strength(0)
-        inverse_delta(0)
-        ice_strength(1)
-        strain_squared(1)
-        stresses(0)
-        strain_squared(2)
-        inverse_delta(1)
-        ice_strength(2)
-        strain_squared(3)
-        inverse_delta(2)
-        stresses(1)
-        ice_strength(3)
-        inverse_delta(3)
-        divergence(0)
-        stresses(2)
-        divergence(1)
-        stresses(3)
-        divergence(2)
-        divergence(3)
+        def last_divergence(c):
+            t = TILES - 1
+            sig1, sig2 = stress[t]
+            east = sbuf(f"east{t}_{c}", [P, P])
+            north = sbuf(f"north{t}_{c}", [P, P])
+            cols = slice(P * c, P * (c + 1))
+            entries = slice(P * c // 16, P * (c + 1) // 16)
+            nc.vector.tensor_tensor(east[:], sig1[:].indirect(est_sb[:, entries]), sig2[:, cols], ALU.subtract)
+            nc.vector.tensor_tensor(north[:], sig2[:].indirect(nor_sb[:, entries]), sig1[:, cols], ALU.subtract)
+            total = bank(f"a{(t + c) % TILES}", f"hid{t}_{c}", [P, P])
+            turn(total[:], east[:], True, False)
+            turn(total[:], north[:], False, True)
+            round_hidden(t, c, total[:])
 
-        for g in range(HALVES):
-            words = hid_t[g][:].rearrange("p c u m e -> p (c u m e)").bitcast(F32)
-            pairs = bank(f"b{g}", f"pairs{g}", [P, 2, 2, P])
-            for c in range(2):
-                for u in range(2):
-                    nc.tensor.transpose(pairs[:, c, u, :], words[:, (2 * c + u) * P : (2 * c + u + 1) * P], ident[:])
-            hid = sbuf(f"hid{g}", [P, HALF * 4], BF16)
-            dst = hid[:].bitcast(F32).rearrange("p (c j u) -> p c j u", c=2, u=2)
-            src = pairs[:].rearrange("p c u j -> p c j u")
-            if g == 0:
-                nc.scalar.copy(dst, src)
-            else:
-                nc.vector.tensor_copy(dst, src)
-            hid_codes = sbuf(f"hid_codes{g}", [P, HALF], U32)
-            hid_plane = sbuf(f"hid_plane{g}", [P, HALF], U8)
+        def modes_of_block(c):
+            words = hid_t[c][:].rearrange("p u m e -> p (u m e)").bitcast(F32)
+            pairs = bank(f"b{c}", f"pairs{c}", [P, 2, P])
+            for u in range(2):
+                nc.tensor.transpose(pairs[:, u, :], words[:, u * P : (u + 1) * P], ident[:])
+            hid = sbuf(f"hid{c}", [P, P * 4], BF16)
+            nc.scalar.copy(hid[:].bitcast(F32).rearrange("p (j u) -> p j u", u=2), pairs[:].rearrange("p u j -> p j u"))
+            hid_codes = sbuf(f"hid_codes{c}", [P, P], U32)
+            hid_plane = sbuf(f"hid_plane{c}", [P, P], U8)
             nc.vector.quantize_mx(out=hid_codes[:].bitcast(FP8X4), scales=hid_plane[:], in_=hid[:])
-            modes = bank(f"b{2 + g}", f"modes{g}", [P, HALF])
+            modes = bank(f"a{(TILES - 1 + c) % TILES}", f"modes{c}", [P, P])
             nc.tensor.matmul_mx(
                 out=modes[:],
                 lhsT=w3_sb[:, 0, :].bitcast(FP4X4),
@@ -268,9 +262,37 @@ def tile_picked_yseaic_div_p_kernel(
                 start=True,
                 stop=True,
             )
-            result = sbuf(f"result{g}", [P, HALF])
-            if g == 0:
-                nc.scalar.copy(result[:], modes[:])
-            else:
-                nc.vector.tensor_copy(result[:], modes[:])
-            nc.sync.dma_start(out=out[:, g * HALF : (g + 1) * HALF], in_=result[:])
+            result = sbuf(f"result{c}", [P, P])
+            nc.vector.tensor_copy(result[:], modes[:])
+            nc.sync.dma_start(out=out[:, c * P : (c + 1) * P], in_=result[:])
+
+        strain_squared(0)
+        nc.scalar.activation(log_sig[:], shared[:], ACT.Ln, bias=LN_FLOOR)
+        for t in range(TILES):
+            ice_thickness(t)
+        inverse_delta(0)
+        strain_squared(1)
+        ice_strength(0)
+        ice_strength(1)
+        strain_squared(2)
+        inverse_delta(1)
+        strain_squared(3)
+        scaled_rates(0)
+        stresses(0)
+        inverse_delta(2)
+        inverse_delta(3)
+        scaled_rates(1)
+        stresses(1)
+        divergence(0)
+        scaled_rates(2)
+        ice_strength(2)
+        ice_strength(3)
+        stresses(2)
+        divergence(1)
+        scaled_rates(3)
+        stresses(3)
+        divergence(2)
+        for c in range(BLOCKS):
+            last_divergence(c)
+        for c in range(BLOCKS):
+            modes_of_block(c)

import math
from contextlib import ExitStack

import concourse.mybir as mybir
from concourse.masks import make_identity

K, T, S, H, N = 1024, 1024, 512, 512, 128
FLOPS = 2 * (2 * K * H * S + H * N * S)

F32 = mybir.dt.float32
BF16 = mybir.dt.bfloat16
I32 = mybir.dt.int32
U32 = mybir.dt.uint32
U16 = mybir.dt.uint16
U8 = mybir.dt.uint8
FP8X4 = mybir.dt.float8_e4m3fn_x4
FP4X4 = mybir.dt.float4_e2m1fn_x4
ALU = mybir.AluOpType
ACT = mybir.ActivationFunctionType

P = 128
PASSES = K // 512
TILES = H // P
BLOCKS = S // P
HALVES = 2
HALF = S // HALVES
LN_FLOOR = 2.0**-60
SQ_N_SLOT = {2: 3, 3: 0}
INV_SLOT = (0, 1, 2, 3)


def tile_picked_yseaic_div_p_kernel(
    tc, x_words, x_scales, w1_words, w1_scales, w2_words, w2_scales, owat, unit, w3_words, w3_scales, offs, est, nor, out
):
    nc = tc.nc
    with ExitStack() as ctx:
        lists = ctx.enter_context(tc.tile_pool(name="lists", bufs=1))
        keep = ctx.enter_context(tc.tile_pool(name="keep", bufs=1))
        psum = ctx.enter_context(tc.psum_pool(name="psum", bufs=1))

        def sbuf(name, shape, dtype=F32, tag=None):
            return keep.tile(shape, dtype, name=name, tag=tag or name, align_bytes=64)

        def bank(tag, name, shape):
            return psum.tile(shape, F32, name=name, tag=tag)

        def load_scale_rows(queue, plane, scales):
            passes = scales.shape[0]
            for q in range(4):
                queue.dma_start(
                    out=plane[32 * q : 32 * q + 4, :].bitcast(I32).rearrange("r (o c) -> r o c", o=passes),
                    in_=scales.bitcast(I32)[:, 4 * q : 4 * q + 4, :].rearrange("o r c -> r o c"),
                )

        def load_fp4_words(queue, name, words):
            passes, width = words.shape[0], words.shape[2]
            tile = sbuf(name, [P, passes, width], U8)
            queue.dma_start(out=tile[:].bitcast(I32), in_=words.bitcast(I32).rearrange("o p c -> p o c"))
            return tile

        offs_sb = lists.tile([P, S // 16], U16, name="offs_sb")
        est_sb = lists.tile([P, S // 16], U16, name="est_sb")
        nor_sb = lists.tile([P, S // 16], U16, name="nor_sb")

        x_plane = sbuf("x_plane", [P, PASSES * T], U8)
        w1_plane = sbuf("w1_plane", [P, PASSES * H], U8)
        w2_plane = sbuf("w2_plane", [P, PASSES * H], U8)
        w3_plane = sbuf("w3_plane", [P, N], U8)
        for plane in (x_plane, w2_plane, w1_plane, w3_plane):
            nc.vector.memset(plane[:].bitcast(I32), 0)

        x_table = [sbuf(f"x_table{o}", [P, T], I32) for o in range(PASSES)]
        water = [sbuf(f"water{g}", [P, 2, S]) for g in range(2)]

        def load_x(o):
            nc.sync.dma_start(out=x_table[o][:], in_=x_words[o].rearrange("p c r -> p (c r)").bitcast(I32))

        load_x(0)
        nc.sync.dma_start(offs_sb[:], offs)
        load_scale_rows(nc.sync, x_plane, x_scales)
        for g in range(2):
            nc.sync.dma_start(out=water[g][:], in_=owat[256 * g : 256 * (g + 1), :].rearrange("(t p) s -> p t s", p=P))
        load_x(1)
        w2_sb = load_fp4_words(nc.sync, "w2_sb", w2_words)
        load_scale_rows(nc.sync, w2_plane, w2_scales)
        nc.sync.dma_start(est_sb[:], est)
        nc.sync.dma_start(nor_sb[:], nor)
        w1_sb = load_fp4_words(nc.sync, "w1_sb", w1_words)
        load_scale_rows(nc.sync, w1_plane, w1_scales)
        unit_sb = sbuf("unit_sb", [P, TILES])
        with nc.allow_non_contiguous_dma(reason="one value a partition and feature tile"):
            nc.sync.dma_start(out=unit_sb[:], in_=unit.rearrange("(t p) o -> p (t o)", p=P))
        w3_sb = load_fp4_words(nc.sync, "w3_sb", w3_words)
        load_scale_rows(nc.sync, w3_plane, w3_scales)

        ident = sbuf("ident", [P, P])
        make_identity(nc, ident[:])

        x_codes = [sbuf(f"x_codes{o}", [P, S], U32) for o in range(PASSES)]
        x_bytes = [sbuf(f"x_bytes{o}", [P, S], U8) for o in range(PASSES)]
        nc.vector.tensor_copy(x_codes[0][:], x_table[0][:].bitcast(U32).indirect(offs_sb[:]))
        for o in range(PASSES):
            nc.vector.tensor_copy(x_bytes[o][:], x_plane[:, o * T : (o + 1) * T].indirect(offs_sb[:]))
        for g in range(HALVES):
            nc.vector.tensor_copy(
                x_codes[1][:, g * HALF : (g + 1) * HALF],
                x_table[1][:].bitcast(U32).indirect(offs_sb[:, g * HALF // 16 : (g + 1) * HALF // 16]),
            )

        vel = [sbuf(f"vel{t}", [P, 2 * S]) for t in range(TILES)]
        for t in range(TILES):
            nc.scalar.activation(vel[t][:, S:], water[t // 2][:, t % 2, :], ACT.Exp, bias=math.log(2.0), scale=-1.0)

        def product(sums, words, plane, t, cols):
            for o in range(PASSES):
                nc.tensor.matmul_mx(
                    out=sums,
                    lhsT=words[:, o, 2 * P * t : 2 * P * (t + 1)].bitcast(FP4X4),
                    lhsT_scale=plane[:, o * H + P * t : o * H + P * (t + 1)],
                    rhs=x_codes[o][:, cols].bitcast(FP8X4),
                    rhs_scale=x_bytes[o][:, cols],
                    start=(o == 0),
                    stop=(o == PASSES - 1),
                )

        vel_plain = [sbuf(f"vel_plain{t}", [P, S]) for t in range(TILES)]
        for g in range(HALVES):
            cols = slice(g * HALF, (g + 1) * HALF)
            ui = bank(("a0", "b3")[g], f"ui0_{g}", [P, HALF])
            product(ui[:], w2_sb, w2_plane, 0, cols)
            nc.scalar.activation(vel[0][:, cols], ui[:], ACT.Sigmoid, scale=2.0)
            nc.vector.tensor_copy(vel_plain[0][:, cols], vel[0][:, cols])
        for t in range(1, TILES):
            ui = bank(f"a{t}", f"ui{t}", [P, S])
            product(ui[:], w2_sb, w2_plane, t, slice(0, S))
            nc.scalar.activation(vel[t][:, :S], ui[:], ACT.Sigmoid, scale=2.0)
            nc.sync.dma_start(out=vel_plain[t][:], in_=vel[t][:, :S])
        hi = [bank(f"b{t}", f"hi{t}", [P, S]) for t in range(TILES)]
        for t in range(TILES):
            product(hi[t][:], w1_sb, w1_plane, t, slice(0, S))
        shared = sbuf("shared", [P, TILES, S])
        for t in range(TILES):
            nc.scalar.activation(shared[:, t, :], hi[t][:], ACT.Sigmoid, scale=-1.0)

        rate_e = [sbuf(f"rate_e{t}", [P, S]) for t in range(TILES)]
        rate_n = [sbuf(f"rate_n{t}", [P, S]) for t in range(TILES)]
        for t in range(TILES):
            nc.vector.tensor_tensor(rate_e[t][:], vel[t][:].indirect(est_sb[:]), vel_plain[t][:], ALU.subtract)
            nc.vector.tensor_tensor(rate_n[t][:], vel[t][:].indirect(nor_sb[:]), vel_plain[t][:], ALU.subtract)

        def turn(dst, src, first, last):
            nc.tensor.matmul(dst, lhsT=src, rhs=ident[:], start=first, stop=last, is_transpose=True)

        strain = {}
        inv_delta = {}
        strength = {}
        log_sig = sbuf("log_sig", [P, TILES, S])
        hid_t = [sbuf(f"hid_t{c}", [P, 2, P, 2], BF16) for c in range(BLOCKS)]
        thickness = {}

        def strain_squared(t):
            if t == 0:
                sq_e, sq_n = sbuf("sq_e0", [P, S])[:], sbuf("sq_n0", [P, S])[:]
            elif t == 1:
                sq_e, sq_n = shared[:, 1, :], shared[:, 2, :]
            else:
                sq_e, sq_n = vel_plain[5 - t][:], shared[:, SQ_N_SLOT[t], :]
            if t < 2:
                nc.scalar.activation(sq_e, rate_e[t][:], ACT.Square)
            else:
                nc.gpsimd.tensor_tensor(sq_e, rate_e[t][:], rate_e[t][:], ALU.mult)
            nc.scalar.activation(sq_n, rate_n[t][:], ACT.Square, scale=0.5)
            strain[t] = bank(f"a{t}", f"strain{t}", [P, BLOCKS, P])
            for i, square in enumerate((sq_e, sq_n)):
                for c in range(BLOCKS):
                    turn(strain[t][:, c, :], square[:, P * c : P * (c + 1)], i == 0 and c == 0, i == 1 and c == BLOCKS - 1)

        def ice_thickness(t):
            thickness[t] = sbuf(f"thickness{t}", [P, S])
            if t == TILES - 1:
                nc.vector.scalar_tensor_tensor(thickness[t][:], log_sig[:, t, :], -1.0, hi[t][:], ALU.mult, ALU.max)
            else:
                nc.vector.scalar_tensor_tensor(thickness[t][:], hi[t][:], -1.0, log_sig[:, t, :], ALU.mult, ALU.min)

        def ice_strength(t):
            strength[t] = sbuf(f"strength{t}", [P, S]) if t < 2 else (rate_n[2], rate_e[2])[t - 2]
            nc.vector.scalar_tensor_tensor(strength[t][:], thickness[t][:], unit_sb[:, t : t + 1], vel[t][:, S:], ALU.mult, ALU.mult)

        def inverse_delta(t):
            slot = INV_SLOT[t]
            nc.scalar.activation(
                shared[:, slot, :], strain[t][:].rearrange("p c f -> p (c f)"), ACT.Abs_reciprocal_sqrt, bias=0.05, scale=4.0
            )
            inv_delta[t] = bank(f"b{t}", f"inv_delta{t}", [P, S])
            for c in range(BLOCKS):
                turn(inv_delta[t][:, P * c : P * (c + 1)], shared[:, slot, P * c : P * (c + 1)], True, True)

        stress = {}

        def scaled_rates(t):
            sig1 = sbuf(f"sig1_{t}", [P, 2 * S])
            sig2 = sbuf(f"sig2_{t}", [P, 2 * S])
            nc.vector.tensor_tensor(sig1[:, S:], inv_delta[t][:], rate_e[t][:], ALU.mult)
            nc.vector.scalar_tensor_tensor(sig2[:, S:], inv_delta[t][:], 0.25, rate_n[t][:], ALU.mult, ALU.mult)
            stress[t] = (sig1, sig2)

        def stresses(t):
            sig1, sig2 = stress[t]
            nc.vector.scalar_tensor_tensor(sig1[:, :S], sig1[:, S:], -0.25, strength[t][:], ALU.add, ALU.mult)
            engine = nc.vector if t == TILES - 1 else nc.gpsimd
            engine.tensor_tensor(sig2[:, :S], sig2[:, S:], strength[t][:], ALU.mult)

        def round_hidden(t, c, total):
            src = total.rearrange("p (m u e) -> p u m e", u=2, e=2)
            nc.scalar.copy(hid_t[c][:, :, 32 * t : 32 * (t + 1), :], src)

        def divergence(t):
            sig1, sig2 = stress[t]
            east = sbuf(f"east{t}", [P, S])
            north = sbuf(f"north{t}", [P, S])
            nc.scalar.activation(east[:], sig1[:].indirect(est_sb[:]), ACT.Copy, scale=-1.0)
            nc.scalar.activation(north[:], sig2[:].indirect(nor_sb[:]), ACT.Copy, scale=-1.0)
            total = bank(f"a{t}", f"hid{t}", [P, BLOCKS, P])
            terms = (sig1, sig2, east, north)
            for i, term in enumerate(terms):
                for c in range(BLOCKS):
                    turn(total[:, c, :], term[:, P * c : P * (c + 1)], i == 0 and c == 0, i == len(terms) - 1 and c == BLOCKS - 1)
            for c in range(BLOCKS):
                round_hidden(t, c, total[:, c, :])

        def last_divergence(c):
            t = TILES - 1
            sig1, sig2 = stress[t]
            east = sbuf(f"east{t}_{c}", [P, P])
            north = sbuf(f"north{t}_{c}", [P, P])
            cols = slice(P * c, P * (c + 1))
            entries = slice(P * c // 16, P * (c + 1) // 16)
            nc.vector.tensor_tensor(east[:], sig1[:].indirect(est_sb[:, entries]), sig2[:, cols], ALU.subtract)
            nc.vector.tensor_tensor(north[:], sig2[:].indirect(nor_sb[:, entries]), sig1[:, cols], ALU.subtract)
            total = bank(f"a{(t + c) % TILES}", f"hid{t}_{c}", [P, P])
            turn(total[:], east[:], True, False)
            turn(total[:], north[:], False, True)
            round_hidden(t, c, total[:])

        def modes_of_block(c):
            words = hid_t[c][:].rearrange("p u m e -> p (u m e)").bitcast(F32)
            pairs = bank(f"b{c}", f"pairs{c}", [P, 2, P])
            for u in range(2):
                nc.tensor.transpose(pairs[:, u, :], words[:, u * P : (u + 1) * P], ident[:])
            hid = sbuf(f"hid{c}", [P, P * 4], BF16)
            nc.scalar.copy(hid[:].bitcast(F32).rearrange("p (j u) -> p j u", u=2), pairs[:].rearrange("p u j -> p j u"))
            hid_codes = sbuf(f"hid_codes{c}", [P, P], U32)
            hid_plane = sbuf(f"hid_plane{c}", [P, P], U8)
            nc.vector.quantize_mx(out=hid_codes[:].bitcast(FP8X4), scales=hid_plane[:], in_=hid[:])
            modes = bank(f"a{(TILES - 1 + c) % TILES}", f"modes{c}", [P, P])
            nc.tensor.matmul_mx(
                out=modes[:],
                lhsT=w3_sb[:, 0, :].bitcast(FP4X4),
                lhsT_scale=w3_plane[:],
                rhs=hid_codes[:].bitcast(FP8X4),
                rhs_scale=hid_plane[:],
                start=True,
                stop=True,
            )
            result = sbuf(f"result{c}", [P, P])
            nc.vector.tensor_copy(result[:], modes[:])
            nc.sync.dma_start(out=out[:, c * P : (c + 1) * P], in_=result[:])

        strain_squared(0)
        nc.scalar.activation(log_sig[:], shared[:], ACT.Ln, bias=LN_FLOOR)
        for t in range(TILES):
            ice_thickness(t)
        inverse_delta(0)
        strain_squared(1)
        ice_strength(0)
        ice_strength(1)
        strain_squared(2)
        inverse_delta(1)
        strain_squared(3)
        scaled_rates(0)
        stresses(0)
        inverse_delta(2)
        inverse_delta(3)
        scaled_rates(1)
        stresses(1)
        divergence(0)
        scaled_rates(2)
        ice_strength(2)
        ice_strength(3)
        stresses(2)
        divergence(1)
        scaled_rates(3)
        stresses(3)
        divergence(2)
        for c in range(BLOCKS):
            last_divergence(c)
        for c in range(BLOCKS):
            modes_of_block(c)
